import numpy as np, ml_dtypes
CORES = [30,158,46,174,86,214]
N = 6
GR, GC = 2, 3
L, KA, KB, F = 12, 4, 6, 64
def setup_inputs(rng):
    return {"a": rng.standard_normal((N, 128, KA * 128), dtype=np.float32).astype(ml_dtypes.bfloat16), "b": rng.standard_normal((N, 128, KB * F), dtype=np.float32).astype(ml_dtypes.bfloat16)}
def reference(a, b):
    A, B = a.astype(np.float64), b.astype(np.float64)
    y = np.zeros((N, 128, F))
    for i in range(GR):
        for j in range(GC):
            for k in range(L):
                At = A[i * GC + k // KA][:, 128 * (k % KA):128 * (k % KA) + 128]
                Bt = B[(k // KB) * GC + j][:, F * (k % KB):F * (k % KB) + F]
                y[i * GC + j] += At.T @ Bt
    return {"y": y.astype(ml_dtypes.bfloat16 if a.dtype != np.float64 else np.float64)}

@@ -1,0 +1,127 @@
+from concourse.bass import DstId, RemoteDMATransfer
+from concourse.mybir import AluOpType
+
+N, GR, GC = 6, 2, 3
+L, KA, KB, F = 12, 4, 6, 64
+P = 128
+
+SCRATCH = {
+    "a_sb": ("sbuf", [P, KA * P], "bfloat16"),
+    "b_sb": ("sbuf", [P, KB * F], "bfloat16"),
+    "b_in": ("sbuf", [P, GC * KA * F], "bfloat16"),
+    "p_out": ("sbuf", [P, GC * F], "bfloat16"),
+    "p_in": ("sbuf", [P, GC * F], "bfloat16"),
+    "t_sb": ("sbuf", [P, F], "float32"),
+    "y_sb": ("sbuf", [P, F], "bfloat16"),
+    "acc0": ("psum", [P, 512], "float32"),
+    "acc1": ("psum", [P, 512], "float32"),
+    "acc2": ("psum", [P, 512], "float32"),
+}
+SEMAPHORES = (["ld_a", "ld_b", "sent", "add1", "add2", "stored"]
+              + ["%s%d" % (n, j) for n in ("bj", "mm", "cp", "pa") for j in range(GC)])
+
+
+def _b_calls(s):
+    r, j = divmod(s, GC)
+    out = []
+    for c in range(GC):
+        k0, k1 = max(KB * r, KA * c), min(KB * (r + 1), KA * (c + 1))
+        dests = [i * GC + c for i in range(GR) if i * GC + c != s]
+        if k0 < k1 and dests:
+            out.append((c == j, (k1 - k0) * len(dests), k0, k1, c, dests))
+    out.sort()
+    return out
+
+
+def _engine_groups(topo, src, dsts):
+    m = topo.mask(src, dsts[0])
+    for d in dsts[1:]:
+        m &= topo.mask(src, d)
+    bits = [e for e in range(m.bit_length()) if (m >> e) & 1]
+    per = 1
+    while per * 2 * len(dsts) <= len(bits):
+        per *= 2
+    return [sum(1 << e for e in bits[n * per:(n + 1) * per]) for n in range(len(dsts))], per
+
+
+def _arrivals(topo, cores, d):
+    need, when = [0] * GC, [0] * GC
+    for s in range(N):
+        done = 0
+        for _, w, _k0, _k1, _c, dests in _b_calls(s):
+            done += w
+            if d in dests:
+                per = _engine_groups(topo, cores[s], [cores[x] for x in dests])[1]
+                need[s % GC] += per
+                when[s % GC] = max(when[s % GC], done)
+    return need, when
+
+
+def rank_program(g, core, T, topo):
+    rank = T.rank_of(core)
+    if rank is None:
+        return
+    cores, S = T.cores, T.sem
+    i, c = divmod(rank, GC)
+    acc = [T.acc0, T.acc1, T.acc2]
+    need, when = _arrivals(topo, cores, rank)
+    travel = sorted((j for j in range(GC) if j != c), key=lambda j: (when[j], j))
+
+    g.sync.dma_start(T.b_sb[:, :], T.b[:, :]).then_inc(S.ld_b, 16)
+    g.sync.dma_start(T.a_sb[:, :], T.a[:, :]).then_inc(S.ld_a, 16)
+
+    g.wait_ge(S.ld_b, 16)
+    sent = 0
+    for _, _w, k0, k1, cc, dests in _b_calls(rank):
+        masks, per = _engine_groups(topo, core, [cores[x] for x in dests])
+        src = T.b_sb[:, F * (k0 - KB * i):F * (k1 - KB * i)]
+        dst = T.b_in[:, F * (c * KA + k0 - KA * cc):F * (c * KA + k1 - KA * cc)]
+        trs = []
+        for x, m in zip(dests, masks):
+            rid, pid = topo.addr(cores[x], core)
+            trs.append(RemoteDMATransfer(dst_ids=[DstId(rid=rid, pnc=pid)], dma_engine_mask=m,
+                                         remote_sem=S["bj%d" % c], src=src, dst=dst))
+            sent += per
+        g.remote_dma_fused(trs, local_sem=S.sent)
+
+    te = g.tensor
+    te.wait_ge(S.ld_a, 16)
+    for j in travel + [c]:
+        if j == c:
+            te.wait_ge(S.ld_b, 16)
+        if need[j]:
+            te.wait_ge(S["bj%d" % j], need[j])
+        for t in range(KA):
+            k = KA * c + t
+            if j == c and k // KB == i:
+                rhs = T.b_sb[:, F * (k - KB * i):F * (k - KB * i) + F]
+            else:
+                rhs = T.b_in[:, F * (j * KA + t):F * (j * KA + t) + F]
+            mm = te.matmul(acc[j][:, 0:F], T.a_sb[:, P * t:P * t + P], rhs, t == 0, t == KA - 1)
+        mm.then_inc(S["mm%d" % j], 1)
+
+    ve = g.vector
+    for j in travel:
+        ve.wait_ge(S["mm%d" % j], 1)
+        ve.tensor_copy(T.p_out[:, F * j:F * j + F], acc[j][:, 0:F]).then_inc(S["cp%d" % j], 1)
+        d = cores[i * GC + j]
+        masks, per = _engine_groups(topo, core, [d])
+        rid, pid = topo.addr(d, core)
+        g.wait_ge(S["cp%d" % j], 1)
+        g.remote_dma(T.p_in[:, F * c:F * c + F], T.p_out[:, F * j:F * j + F], S["pa%d" % c], S.sent, pid, rid, masks[0])
+        sent += per
+    g.wait_ge(S.sent, sent)
+
+    srcs = sorted((cc for cc in range(GC) if cc != c), key=lambda cc: (_arrivals(topo, cores, i * GC + cc)[1][c], cc))
+    ve.wait_ge(S["mm%d" % c], 1)
+    for n, cc in enumerate(srcs):
+        per = _engine_groups(topo, cores[i * GC + cc], [core])[1]
+        ve.wait_ge(S["pa%d" % cc], per)
+        if n == 0:
+            ve.tensor_tensor(T.t_sb[:, :], acc[c][:, 0:F], T.p_in[:, F * cc:F * cc + F], AluOpType.add).then_inc(S.add1, 1)
+            ve.wait_ge(S.add1, 1)
+        else:
+            ve.tensor_tensor(T.y_sb[:, :], T.t_sb[:, :], T.p_in[:, F * cc:F * cc + F], AluOpType.add).then_inc(S.add2, 1)
+    g.sync.wait_ge(S.add2, 1)
+    g.sync.dma_start(T.y[:, :], T.y_sb[:, :]).then_inc(S.stored, 16)
+    g.sync.wait_ge(S.stored, 16)

@@ -1,60 +1,59 @@
-from concourse.bass import DstId, RemoteDMATransfer
 from concourse.mybir import AluOpType
 
 N, GR, GC = 6, 2, 3
 L, KA, KB, F = 12, 4, 6, 64
 P = 128
+P_OF = [[2, 0, 1], [1, 2, 0]]
 
 SCRATCH = {
     "a_sb": ("sbuf", [P, KA * P], "bfloat16"),
+    "a_in": ("sbuf", [P, KA * P], "bfloat16"),
     "b_sb": ("sbuf", [P, KB * F], "bfloat16"),
-    "b_in": ("sbuf", [P, GC * KA * F], "bfloat16"),
-    "p_out": ("sbuf", [P, GC * F], "bfloat16"),
-    "p_in": ("sbuf", [P, GC * F], "bfloat16"),
-    "t_sb": ("sbuf", [P, F], "float32"),
+    "b_col": ("sbuf", [P, KB * F], "bfloat16"),
+    "b_duty": ("sbuf", [P, KA * F], "bfloat16"),
+    "p_out": ("sbuf", [P, F], "bfloat16"),
+    "p_in": ("sbuf", [P, F], "bfloat16"),
     "y_sb": ("sbuf", [P, F], "bfloat16"),
     "acc0": ("psum", [P, 512], "float32"),
     "acc1": ("psum", [P, 512], "float32"),
-    "acc2": ("psum", [P, 512], "float32"),
 }
-SEMAPHORES = (["ld_a", "ld_b", "sent", "add1", "add2", "stored"]
-              + ["%s%d" % (n, j) for n in ("bj", "mm", "cp", "pa") for j in range(GC)])
+SEMAPHORES = ["ld_a", "ld_b", "sent", "bd", "bc", "ra", "pa", "mmd", "mml", "cp", "add", "stored"]
 
 
-def _b_calls(s):
-    r, j = divmod(s, GC)
-    out = []
-    for c in range(GC):
-        k0, k1 = max(KB * r, KA * c), min(KB * (r + 1), KA * (c + 1))
-        dests = [i * GC + c for i in range(GR) if i * GC + c != s]
-        if k0 < k1 and dests:
-            out.append((c == j, (k1 - k0) * len(dests), k0, k1, c, dests))
-    out.sort()
-    return out
-
-
-def _engine_groups(topo, src, dsts):
-    m = topo.mask(src, dsts[0])
-    for d in dsts[1:]:
-        m &= topo.mask(src, d)
+def _engines(topo, src, dst):
+    m = topo.mask(src, dst)
     bits = [e for e in range(m.bit_length()) if (m >> e) & 1]
-    per = 1
-    while per * 2 * len(dsts) <= len(bits):
-        per *= 2
-    return [sum(1 << e for e in bits[n * per:(n + 1) * per]) for n in range(len(dsts))], per
+    n = 1
+    while n * 2 <= len(bits):
+        n *= 2
+    return sum(1 << e for e in bits[:n]), n
 
 
-def _arrivals(topo, cores, d):
-    need, when = [0] * GC, [0] * GC
-    for s in range(N):
-        done = 0
-        for _, w, _k0, _k1, _c, dests in _b_calls(s):
-            done += w
-            if d in dests:
-                per = _engine_groups(topo, cores[s], [cores[x] for x in dests])[1]
-                need[s % GC] += per
-                when[s % GC] = max(when[s % GC], done)
-    return need, when
+def _local_blocks(i, j):
+    return [j] + [c for c in range(GC) if c != j and c != P_OF[i][j]]
+
+
+def _b_sends(s):
+    r, q = divmod(s, GC)
+    duty = []
+    for i in range(GR):
+        c = P_OF[i][q]
+        k0, k1 = max(KB * r, KA * c), min(KB * (r + 1), KA * (c + 1))
+        if k0 < k1:
+            duty.append((k1 - k0, "bd", k0, k1, i * GC + c))
+    duty.sort()
+    out = [x[1:] for x in duty]
+    for i in range(GR):
+        if i == r:
+            continue
+        ks = [k for k in range(KB * r, KB * (r + 1)) if k // KA in _local_blocks(i, q)]
+        while ks:
+            n = 1
+            while n < len(ks) and ks[n] == ks[0] + n:
+                n += 1
+            out.append(("bc", ks[0], ks[0] + n, i * GC + q))
+            ks = ks[n:]
+    return out
 
 
 def rank_program(g, core, T, topo):
@@ -62,66 +61,77 @@ def rank_program(g, core, T, topo):
     if rank is None:
         return
     cores, S = T.cores, T.sem
-    i, c = divmod(rank, GC)
-    acc = [T.acc0, T.acc1, T.acc2]
-    need, when = _arrivals(topo, cores, rank)
-    travel = sorted((j for j in range(GC) if j != c), key=lambda j: (when[j], j))
+    i, j = divmod(rank, GC)
+    te, ve = g.tensor, g.vector
+    sent = [0]
+
+    def send(x, dst, src, sem):
+        m, n = _engines(topo, core, cores[x])
+        rid, pid = topo.addr(cores[x], core)
+        g.remote_dma(dst, src, sem, S.sent, pid, rid, m)
+        sent[0] += n
+
+    need = {"bd": 0, "bc": 0}
+    for s in range(N):
+        for kind, _k0, _k1, d in _b_sends(s):
+            if d == rank:
+                need[kind] += _engines(topo, cores[s], core)[1]
+    fetched = _local_blocks(i, j)[1]
+    a_to = [x for x in range(GC) if x != j and _local_blocks(i, x)[1] == j][0]
+    duty_j = [x for x in range(GC) if P_OF[i][x] == j][0]
 
     g.sync.dma_start(T.b_sb[:, :], T.b[:, :]).then_inc(S.ld_b, 16)
     g.sync.dma_start(T.a_sb[:, :], T.a[:, :]).then_inc(S.ld_a, 16)
 
     g.wait_ge(S.ld_b, 16)
-    sent = 0
-    for _, _w, k0, k1, cc, dests in _b_calls(rank):
-        masks, per = _engine_groups(topo, core, [cores[x] for x in dests])
+    for kind, k0, k1, d in _b_sends(rank):
         src = T.b_sb[:, F * (k0 - KB * i):F * (k1 - KB * i)]
-        dst = T.b_in[:, F * (c * KA + k0 - KA * cc):F * (c * KA + k1 - KA * cc)]
-        trs = []
-        for x, m in zip(dests, masks):
-            rid, pid = topo.addr(cores[x], core)
-            trs.append(RemoteDMATransfer(dst_ids=[DstId(rid=rid, pnc=pid)], dma_engine_mask=m,
-                                         remote_sem=S["bj%d" % c], src=src, dst=dst))
-            sent += per
-        g.remote_dma_fused(trs, local_sem=S.sent)
-
-    te = g.tensor
-    te.wait_ge(S.ld_a, 16)
-    for j in travel + [c]:
-        if j == c:
-            te.wait_ge(S.ld_b, 16)
-        if need[j]:
-            te.wait_ge(S["bj%d" % j], need[j])
-        for t in range(KA):
-            k = KA * c + t
-            if j == c and k // KB == i:
-                rhs = T.b_sb[:, F * (k - KB * i):F * (k - KB * i) + F]
-            else:
-                rhs = T.b_in[:, F * (j * KA + t):F * (j * KA + t) + F]
-            mm = te.matmul(acc[j][:, 0:F], T.a_sb[:, P * t:P * t + P], rhs, t == 0, t == KA - 1)
-        mm.then_inc(S["mm%d" % j], 1)
-
-    ve = g.vector
-    for j in travel:
-        ve.wait_ge(S["mm%d" % j], 1)
-        ve.tensor_copy(T.p_out[:, F * j:F * j + F], acc[j][:, 0:F]).then_inc(S["cp%d" % j], 1)
-        d = cores[i * GC + j]
-        masks, per = _engine_groups(topo, core, [d])
-        rid, pid = topo.addr(d, core)
-        g.wait_ge(S["cp%d" % j], 1)
-        g.remote_dma(T.p_in[:, F * c:F * c + F], T.p_out[:, F * j:F * j + F], S["pa%d" % c], S.sent, pid, rid, masks[0])
-        sent += per
-    g.wait_ge(S.sent, sent)
-
-    srcs = sorted((cc for cc in range(GC) if cc != c), key=lambda cc: (_arrivals(topo, cores, i * GC + cc)[1][c], cc))
-    ve.wait_ge(S["mm%d" % c], 1)
-    for n, cc in enumerate(srcs):
-        per = _engine_groups(topo, cores[i * GC + cc], [core])[1]
-        ve.wait_ge(S["pa%d" % cc], per)
-        if n == 0:
-            ve.tensor_tensor(T.t_sb[:, :], acc[c][:, 0:F], T.p_in[:, F * cc:F * cc + F], AluOpType.add).then_inc(S.add1, 1)
-            ve.wait_ge(S.add1, 1)
+        if kind == "bd":
+            base = KA * (d % GC)
+            send(d, T.b_duty[:, F * (k0 - base):F * (k1 - base)], src, S.bd)
         else:
-            ve.tensor_tensor(T.y_sb[:, :], T.t_sb[:, :], T.p_in[:, F * cc:F * cc + F], AluOpType.add).then_inc(S.add2, 1)
-    g.sync.wait_ge(S.add2, 1)
+            send(d, T.b_col[:, F * (k0 - KB * i):F * (k1 - KB * i)], src, S.bc)
+    g.wait_ge(S.ld_a, 16)
+    send(i * GC + a_to, T.a_in[:, :], T.a_sb[:, :], S.ra)
+
+    def b_tile(k):
+        buf = T.b_sb if k // KB == i else T.b_col
+        return buf[:, F * (k % KB):F * (k % KB) + F]
+
+    own = [k for k in range(KA * j, KA * j + KA)]
+    fet = [k for k in range(KA * fetched, KA * fetched + KA)]
+    early = [k for k in own if k // KB == i]
+    late = [k for k in own if k // KB != i] + fet
+    n_loc = len(early) + len(late)
+    te.wait_ge(S.ld_a, 16)
+    te.wait_ge(S.ld_b, 16)
+    done = 0
+    for k in early:
+        te.matmul(T.acc0[:, 0:F], T.a_sb[:, P * (k - KA * j):P * (k - KA * j) + P], b_tile(k), done == 0, done == n_loc - 1)
+        done += 1
+    te.wait_ge(S.bd, need["bd"])
+    for t in range(KA):
+        mm = te.matmul(T.acc1[:, 0:F], T.a_sb[:, P * t:P * t + P], T.b_duty[:, F * t:F * t + F], t == 0, t == KA - 1)
+    mm.then_inc(S.mmd, 1)
+    if need["bc"]:
+        te.wait_ge(S.bc, need["bc"])
+    for k in late:
+        if k == fet[0]:
+            te.wait_ge(S.ra, _engines(topo, cores[i * GC + fetched], core)[1])
+        lhs = T.a_sb[:, P * (k - KA * j):P * (k - KA * j) + P] if k in own else T.a_in[:, P * (k - KA * fetched):P * (k - KA * fetched) + P]
+        mm = te.matmul(T.acc0[:, 0:F], lhs, b_tile(k), done == 0, done == n_loc - 1)
+        done += 1
+    mm.then_inc(S.mml, 1)
+
+    ve.wait_ge(S.mmd, 1)
+    ve.tensor_copy(T.p_out[:, :], T.acc1[:, 0:F]).then_inc(S.cp, 1)
+    g.wait_ge(S.cp, 1)
+    send(i * GC + duty_j, T.p_in[:, :], T.p_out[:, :], S.pa)
+    g.wait_ge(S.sent, sent[0])
+
+    ve.wait_ge(S.mml, 1)
+    ve.wait_ge(S.pa, _engines(topo, cores[i * GC + P_OF[i][j]], core)[1])
+    ve.tensor_tensor(T.y_sb[:, :], T.acc0[:, 0:F], T.p_in[:, :], AluOpType.add).then_inc(S.add, 1)
+    g.sync.wait_ge(S.add, 1)
     g.sync.dma_start(T.y[:, :], T.y_sb[:, :]).then_inc(S.stored, 16)
     g.sync.wait_ge(S.stored, 16)

from concourse.mybir import AluOpType

N, GR, GC = 6, 2, 3
L, KA, KB, F = 12, 4, 6, 64
P = 128
P_OF = [[2, 0, 1], [1, 2, 0]]

SCRATCH = {
    "a_sb": ("sbuf", [P, KA * P], "bfloat16"),
    "a_in": ("sbuf", [P, KA * P], "bfloat16"),
    "b_sb": ("sbuf", [P, KB * F], "bfloat16"),
    "b_col": ("sbuf", [P, KB * F], "bfloat16"),
    "b_duty": ("sbuf", [P, KA * F], "bfloat16"),
    "p_out": ("sbuf", [P, F], "bfloat16"),
    "p_in": ("sbuf", [P, F], "bfloat16"),
    "y_sb": ("sbuf", [P, F], "bfloat16"),
    "acc0": ("psum", [P, 512], "float32"),
    "acc1": ("psum", [P, 512], "float32"),
}
SEMAPHORES = ["ld_a", "ld_b", "sent", "bd", "bc", "ra", "pa", "mmd", "mml", "cp", "add", "stored"]


def _engines(topo, src, dst):
    m = topo.mask(src, dst)
    bits = [e for e in range(m.bit_length()) if (m >> e) & 1]
    n = 1
    while n * 2 <= len(bits):
        n *= 2
    return sum(1 << e for e in bits[:n]), n


def _local_blocks(i, j):
    return [j] + [c for c in range(GC) if c != j and c != P_OF[i][j]]


def _b_sends(s):
    r, q = divmod(s, GC)
    duty = []
    for i in range(GR):
        c = P_OF[i][q]
        k0, k1 = max(KB * r, KA * c), min(KB * (r + 1), KA * (c + 1))
        if k0 < k1:
            duty.append((k1 - k0, "bd", k0, k1, i * GC + c))
    duty.sort()
    out = [x[1:] for x in duty]
    for i in range(GR):
        if i == r:
            continue
        ks = [k for k in range(KB * r, KB * (r + 1)) if k // KA in _local_blocks(i, q)]
        while ks:
            n = 1
            while n < len(ks) and ks[n] == ks[0] + n:
                n += 1
            out.append(("bc", ks[0], ks[0] + n, i * GC + q))
            ks = ks[n:]
    return out


def rank_program(g, core, T, topo):
    rank = T.rank_of(core)
    if rank is None:
        return
    cores, S = T.cores, T.sem
    i, j = divmod(rank, GC)
    te, ve = g.tensor, g.vector
    sent = [0]

    def send(x, dst, src, sem):
        m, n = _engines(topo, core, cores[x])
        rid, pid = topo.addr(cores[x], core)
        g.remote_dma(dst, src, sem, S.sent, pid, rid, m)
        sent[0] += n

    need = {"bd": 0, "bc": 0}
    for s in range(N):
        for kind, _k0, _k1, d in _b_sends(s):
            if d == rank:
                need[kind] += _engines(topo, cores[s], core)[1]
    fetched = _local_blocks(i, j)[1]
    a_to = [x for x in range(GC) if x != j and _local_blocks(i, x)[1] == j][0]
    duty_j = [x for x in range(GC) if P_OF[i][x] == j][0]

    g.sync.dma_start(T.b_sb[:, :], T.b[:, :]).then_inc(S.ld_b, 16)
    g.sync.dma_start(T.a_sb[:, :], T.a[:, :]).then_inc(S.ld_a, 16)

    g.wait_ge(S.ld_b, 16)
    for kind, k0, k1, d in _b_sends(rank):
        src = T.b_sb[:, F * (k0 - KB * i):F * (k1 - KB * i)]
        if kind == "bd":
            base = KA * (d % GC)
            send(d, T.b_duty[:, F * (k0 - base):F * (k1 - base)], src, S.bd)
        else:
            send(d, T.b_col[:, F * (k0 - KB * i):F * (k1 - KB * i)], src, S.bc)
    g.wait_ge(S.ld_a, 16)
    send(i * GC + a_to, T.a_in[:, :], T.a_sb[:, :], S.ra)

    def b_tile(k):
        buf = T.b_sb if k // KB == i else T.b_col
        return buf[:, F * (k % KB):F * (k % KB) + F]

    own = [k for k in range(KA * j, KA * j + KA)]
    fet = [k for k in range(KA * fetched, KA * fetched + KA)]
    early = [k for k in own if k // KB == i]
    late = [k for k in own if k // KB != i] + fet
    n_loc = len(early) + len(late)
    te.wait_ge(S.ld_a, 16)
    te.wait_ge(S.ld_b, 16)
    done = 0
    for k in early:
        te.matmul(T.acc0[:, 0:F], T.a_sb[:, P * (k - KA * j):P * (k - KA * j) + P], b_tile(k), done == 0, done == n_loc - 1)
        done += 1
    te.wait_ge(S.bd, need["bd"])
    for t in range(KA):
        mm = te.matmul(T.acc1[:, 0:F], T.a_sb[:, P * t:P * t + P], T.b_duty[:, F * t:F * t + F], t == 0, t == KA - 1)
    mm.then_inc(S.mmd, 1)
    if need["bc"]:
        te.wait_ge(S.bc, need["bc"])
    for k in late:
        if k == fet[0]:
            te.wait_ge(S.ra, _engines(topo, cores[i * GC + fetched], core)[1])
        lhs = T.a_sb[:, P * (k - KA * j):P * (k - KA * j) + P] if k in own else T.a_in[:, P * (k - KA * fetched):P * (k - KA * fetched) + P]
        mm = te.matmul(T.acc0[:, 0:F], lhs, b_tile(k), done == 0, done == n_loc - 1)
        done += 1
    mm.then_inc(S.mml, 1)

    ve.wait_ge(S.mmd, 1)
    ve.tensor_copy(T.p_out[:, :], T.acc1[:, 0:F]).then_inc(S.cp, 1)
    g.wait_ge(S.cp, 1)
    send(i * GC + duty_j, T.p_in[:, :], T.p_out[:, :], S.pa)
    g.wait_ge(S.sent, sent[0])

    ve.wait_ge(S.mml, 1)
    ve.wait_ge(S.pa, _engines(topo, cores[i * GC + P_OF[i][j]], core)[1])
    ve.tensor_tensor(T.y_sb[:, :], T.acc0[:, 0:F], T.p_in[:, :], AluOpType.add).then_inc(S.add, 1)
    g.sync.wait_ge(S.add, 1)
    g.sync.dma_start(T.y[:, :], T.y_sb[:, :]).then_inc(S.stored, 16)
    g.sync.wait_ge(S.stored, 16)
